import numpy as np
import ml_dtypes


def mxq(x, axis, fmt="e4m3"):
    dtype, down = {"e4m3": (ml_dtypes.float8_e4m3fn, 7), "e5m2": (ml_dtypes.float8_e5m2, 14)}[fmt]
    v = np.moveaxis(np.asarray(x, np.float32).astype(ml_dtypes.bfloat16).astype(np.float64), axis, -1)
    blocks = v.reshape(v.shape[:-1] + (-1, 32))
    amax = np.abs(blocks).max(-1, keepdims=True)
    byte = np.maximum(np.where(amax > 0, np.frexp(amax)[1] - 1 + 127, 0) - down, 1)
    scale = np.exp2(byte - 127.0)
    codes = (blocks / scale).astype(np.float32).astype(dtype).astype(np.float64)
    return np.moveaxis((codes * scale).reshape(v.shape), -1, axis)


WIDE = False


def mx_kscale(k, group=512):
    if not WIDE:
        return np.ones(k)
    levels = np.array([18, -18])
    if group != 512:
        return np.exp2(np.random.permutation(np.resize(levels, k // group))).repeat(group)
    if k % 512:
        return np.exp2(np.random.permutation(np.resize(levels, k // 32))).repeat(32)
    a = np.empty((k // 512, 16))
    for p in range(k // 512):
        a[p, :8] = np.random.permutation(np.resize(levels, 8))
        for g in range(8):
            far = levels[np.abs(levels - a[p, g]) >= 10]
            a[p, g + 8] = far[np.random.randint(len(far))]
    return np.exp2(a.ravel()).repeat(32)


def f64(x):
    return np.asarray(x).astype(np.float64)


def sigmoid(v):
    return 1.0 / (1.0 + np.exp(-v))


def silu(v):
    return v / (1.0 + np.exp(-v))


G, D, M, N = 4, 128, 128, 512


def setup_inputs():
    n = np.random.standard_normal
    s_d = mx_kscale(D, 0)
    return {
        "x": (n((G, D, N)) * s_d[:, None]).astype(np.float32),
        "w1": (n((G, D, M)) / np.sqrt(D) / s_d[:, None]).astype(np.float32),
        "w2": (n((G, D, M)) / np.sqrt(D) / s_d[:, None]).astype(np.float32),
        "sh": (np.random.uniform(0.1, 0.4, (G, M, 1))).astype(np.float32),
        "d0": (np.random.uniform(5.0, 9.0, (G, M, N))).astype(np.float32),
        "dx": (n((G, D, N)) * s_d[:, None]).astype(np.float32),
        "og": (np.random.uniform(0.5, 2.0, (G, M, 1))).astype(np.float32),
        "base": (0.3 * n((G, M, N))).astype(np.float32),
    }


def reference(x, w1, w2, sh, d0, dx, og, base):
    w1q = mxq(f64(w1), 1, "e4m3")
    xq = mxq(f64(x), 1, "e4m3")
    z1 = w1q.transpose(0, 2, 1) @ xq
    dxq = mxq(f64(dx), 1, "e4m3")
    tz1 = w1q.transpose(0, 2, 1) @ dxq
    w2q = mxq(f64(w2), 1, "e4m3")
    z2 = w2q.transpose(0, 2, 1) @ xq
    tz2 = w2q.transpose(0, 2, 1) @ dxq
    q1 = f64(d0) - z1
    xq1 = tz1 * (-1.0)
    xh = (tz2 * sigmoid(z2) * (1.0 + z2 * (1.0 - sigmoid(z2))) - xq1 * f64(sh) * silu(z2) / (q1 * f64(sh) + 1.0)) / (q1 * f64(sh) + 1.0)
    y = xh * f64(og) + f64(base)
    return y

@@ -1,0 +1,267 @@
+from contextlib import ExitStack
+
+import concourse.mybir as mybir
+
+G, D, M, N = 4, 128, 128, 512
+FLOPS = 4 * 2 * G * D * M * N
+
+F32 = mybir.dt.float32
+BF16 = mybir.dt.bfloat16
+U32 = mybir.dt.uint32
+U8 = mybir.dt.uint8
+FP8X4 = mybir.dt.float8_e4m3fn_x4
+ACT = mybir.ActivationFunctionType
+ALU = mybir.AluOpType
+
+P = 128
+PACK = 4
+ROWS = D // PACK
+HALF = N // 2
+MM_N = 128
+RUN = 4
+
+
+def tile_rows_tnkernstudent_kernel(tc, x, w1, w2, sh, d0, dx, og, base, out):
+    nc = tc.nc
+    halves = [slice(0, HALF), slice(HALF, N)]
+    whole = slice(0, N)
+
+    with ExitStack() as ctx:
+        sb = ctx.enter_context(tc.tile_pool(name="sb", bufs=1))
+        ps = ctx.enter_context(tc.psum_pool(name="ps", bufs=1))
+        ctx.enter_context(tc.manual_schedule())
+
+        def per_group(name):
+            return [sb.tile([P, N], F32, name="%s%d" % (name, g)) for g in range(G)]
+
+        def operand(name, width):
+            return {
+                "raw": sb.tile([P, PACK, width], F32, name=name + "_raw", align_bytes=64),
+                "bf16": sb.tile([P, width, PACK], BF16, name=name + "_bf16", align_bytes=64),
+                "codes": sb.tile([P, width], U32, name=name + "_codes", align_bytes=64),
+                "scales": sb.tile([P, width], U8, name=name + "_scales", align_bytes=64),
+            }
+
+        def load_operand(op, src, cols):
+            nc.sync.dma_start(out=op["raw"][:], in_=src.rearrange("g (p j) n -> (g p) j n", j=PACK)[:, :, cols])
+
+        def interleave_views(op):
+            dst = op["bf16"][:].rearrange("p (c i) j -> p c j i", i=RUN)
+            src = op["raw"][:].rearrange("p j (c i) -> p c j i", i=RUN)
+            return dst, src
+
+        def interleave_v(op):
+            dst, src = interleave_views(op)
+            nc.vector.tensor_copy(out=dst, in_=src)
+
+        def interleave_s(op):
+            dst, src = interleave_views(op)
+            nc.scalar.copy(out=dst, in_=src)
+
+        def quantize(op):
+            nc.vector.quantize_mx(
+                out=op["codes"][:].bitcast(FP8X4),
+                scales=op["scales"][:],
+                in_=op["bf16"][:].rearrange("p n j -> p (n j)"),
+            )
+
+        def product(bank, g, w_op, x_ops, h):
+            rows = slice(ROWS * g, ROWS * (g + 1))
+            for c in range(0, HALF, MM_N):
+                nc.tensor.matmul_mx(
+                    out=bank[:, h * HALF + c : h * HALF + c + MM_N],
+                    lhsT=w_op["codes"][rows, :].bitcast(FP8X4),
+                    lhsT_scale=w_op["scales"][rows, :],
+                    rhs=x_ops[h]["codes"][rows, c : c + MM_N].bitcast(FP8X4),
+                    rhs_scale=x_ops[h]["scales"][rows, c : c + MM_N],
+                    start=True,
+                    stop=True,
+                )
+
+        xq = [operand("x%d" % h, HALF) for h in range(2)]
+        dxq = [operand("dx%d" % h, HALF) for h in range(2)]
+        w1q = operand("w1", M)
+        w2q = operand("w2", M)
+        bank_a = [ps.tile([P, N], F32, name="bank_a%d" % g) for g in range(G)]
+        bank_b = [ps.tile([P, N], F32, name="bank_b%d" % g) for g in range(G)]
+        d0_pairs = [sb.tile([P, 2, N], F32, name="d0_pair%d" % i) for i in range(2)]
+        base_pairs = [sb.tile([P, 2, N], F32, name="base_pair%d" % i) for i in range(2)]
+        vec_rows = sb.tile([P, 2 * M], F32, name="vec_rows", align_bytes=64)
+        vec_cols = sb.tile([P, 2 * M], F32, name="vec_cols", align_bytes=64)
+        sh_half = sb.tile([P, G], F32, name="sh_half")
+        e0 = per_group("e0")
+        dn = per_group("dn")
+        nsilu = per_group("nsilu")
+        tanh = per_group("tanh")
+        silu = per_group("silu")
+        a1 = per_group("a1")
+        a2 = per_group("a2")
+        bterm = per_group("bterm")
+        root = per_group("root")
+        inv = per_group("inv")
+        inv2 = per_group("inv2")
+        ad = per_group("ad")
+        total = per_group("total")
+        scaled = per_group("scaled")
+        y = per_group("y")
+
+        def sh_col(g):
+            return vec_cols[:, 32 * g : 32 * g + 1]
+
+        def og_col(g):
+            return vec_cols[:, M + 32 * g : M + 32 * g + 1]
+
+        nc.gpsimd.memset(vec_rows[:], 0.0)
+        load_operand(xq[0], x, halves[0])
+        load_operand(w2q, w2, slice(0, M))
+        for i, vec in enumerate((sh, og)):
+            nc.sync.dma_start(
+                out=vec_rows[0:P:32, i * M : (i + 1) * M].rearrange("a (g i) -> a g i", i=32),
+                in_=vec.rearrange("g (a i) o -> a g (i o)", i=32),
+            )
+        load_operand(w1q, w1, slice(0, M))
+        load_operand(xq[1], x, halves[1])
+        for i in range(2):
+            nc.sync.dma_start(out=d0_pairs[i][:], in_=d0[2 * i : 2 * i + 2].rearrange("g m n -> m g n"))
+        for h in range(2):
+            load_operand(dxq[h], dx, halves[h])
+        for i in range(2):
+            nc.sync.dma_start(out=base_pairs[i][:], in_=base[2 * i : 2 * i + 2].rearrange("g m n -> m g n"))
+
+        def z2_functions(g, cols):
+            z2 = bank_b[g][:, cols]
+            nc.scalar.activation(out=nsilu[g][:, cols], in_=z2, func=ACT.Silu, scale=-1.0)
+            nc.scalar.activation(out=tanh[g][:, cols], in_=z2, func=ACT.Tanh, scale=0.5)
+            nc.scalar.activation(out=silu[g][:, cols], in_=z2, func=ACT.Silu)
+
+        def make_e0(g):
+            nc.gpsimd.tensor_scalar(
+                out=e0[g][:], in0=d0_pairs[g // 2][:, g % 2, :], scalar1=sh_half[:, g : g + 1], scalar2=0.5,
+                op0=ALU.mult, op1=ALU.add,
+            )
+
+        def make_dn(g):
+            nc.vector.scalar_tensor_tensor(
+                out=dn[g][:], in0=bank_a[g][:], scalar=sh_half[:, g : g + 1], in1=e0[g][:],
+                op0=ALU.mult, op1=ALU.subtract,
+            )
+
+        def make_a2(g):
+            nc.vector.scalar_tensor_tensor(
+                out=a2[g][:], in0=tanh[g][:], scalar=1.0, in1=dn[g][:], op0=ALU.add, op1=ALU.mult
+            )
+
+        def make_a1(g, cols):
+            nc.vector.scalar_tensor_tensor(
+                out=a1[g][:, cols], in0=nsilu[g][:, cols], scalar=1.0, in1=bank_a[g][:, cols],
+                op0=ALU.subtract, op1=ALU.mult,
+            )
+
+        def make_b(g, cols):
+            nc.vector.scalar_tensor_tensor(
+                out=bterm[g][:, cols], in0=bank_b[g][:, cols], scalar=sh_col(g), in1=silu[g][:, cols],
+                op0=ALU.mult, op1=ALU.mult,
+            )
+
+        def make_ad(g):
+            nc.vector.tensor_tensor(out=ad[g][:], in0=a1[g][:], in1=a2[g][:], op=ALU.mult)
+
+        def make_total(g):
+            nc.vector.tensor_tensor(out=total[g][:], in0=ad[g][:], in1=bterm[g][:], op=ALU.add)
+
+        def make_scaled(g):
+            nc.vector.scalar_tensor_tensor(
+                out=scaled[g][:], in0=total[g][:], scalar=og_col(g), in1=inv2[g][:], op0=ALU.mult, op1=ALU.mult
+            )
+
+        def make_y(g):
+            nc.vector.tensor_tensor(out=y[g][:], in0=scaled[g][:], in1=base_pairs[g // 2][:, g % 2, :], op=ALU.add)
+            nc.sync.dma_start(out=out[g], in_=y[g][:])
+
+        interleave_v(xq[0])
+        interleave_v(w2q)
+        quantize(xq[0])
+        quantize(w2q)
+        for g in range(G):
+            product(bank_b[g], g, w2q, xq, 0)
+        interleave_v(w1q)
+        nc.vector.transpose(vec_cols[:], vec_rows[:])
+        quantize(w1q)
+        nc.vector.tensor_scalar(out=sh_half[:], in0=vec_cols[:, 0:M:32], scalar1=0.5, scalar2=None, op0=ALU.mult)
+        for g in range(G):
+            product(bank_a[g], g, w1q, xq, 0)
+        z2_functions(0, halves[0])
+        z2_functions(1, halves[0])
+        interleave_v(xq[1])
+        quantize(xq[1])
+        for g in range(2):
+            product(bank_a[g], g, w1q, xq, 1)
+        for g in range(G):
+            product(bank_b[g], g, w2q, xq, 1)
+        for g in range(2, G):
+            product(bank_a[g], g, w1q, xq, 1)
+        z2_functions(0, halves[1])
+        z2_functions(1, halves[1])
+        for g in range(G):
+            make_e0(g)
+
+        make_dn(0)
+        make_dn(1)
+        make_a2(0)
+        make_dn(2)
+        make_dn(3)
+        interleave_s(dxq[0])
+        interleave_s(dxq[1])
+        z2_functions(2, whole)
+        z2_functions(3, whole)
+        quantize(dxq[0])
+        for g in range(2):
+            product(bank_a[g], g, w2q, dxq, 0)
+            product(bank_b[g], g, w1q, dxq, 0)
+        make_a2(1)
+        make_a1(0, halves[0])
+        make_b(0, halves[0])
+        make_a1(1, halves[0])
+        quantize(dxq[1])
+        make_b(1, halves[0])
+        for g in range(2):
+            product(bank_a[g], g, w2q, dxq, 1)
+            product(bank_b[g], g, w1q, dxq, 1)
+        for g in range(2, G):
+            for h in range(2):
+                product(bank_a[g], g, w2q, dxq, h)
+        for g in range(2, G):
+            for h in range(2):
+                product(bank_b[g], g, w1q, dxq, h)
+        for g in range(2):
+            make_a1(g, halves[1])
+            make_b(g, halves[1])
+
+        for pair in ((0, 1), (2, 3)):
+            for g in pair:
+                nc.scalar.activation(out=root[g][:], in_=dn[g][:], func=ACT.Abs_reciprocal_sqrt, scale=2.0)
+            for g in pair:
+                nc.scalar.activation(out=inv[g][:], in_=root[g][:], func=ACT.Square)
+            for g in pair:
+                nc.scalar.activation(out=inv2[g][:], in_=inv[g][:], func=ACT.Square)
+
+        make_ad(0)
+        make_ad(1)
+        make_total(0)
+        make_total(1)
+        for g in range(2, G):
+            make_a2(g)
+            make_a1(g, whole)
+            make_b(g, whole)
+        make_ad(2)
+        make_scaled(0)
+        make_ad(3)
+        make_y(0)
+        make_total(2)
+        make_scaled(1)
+        make_total(3)
+        make_y(1)
+        make_scaled(2)
+        make_scaled(3)
+        make_y(2)
+        make_y(3)

@@ -65,18 +65,19 @@ def tile_rows_tnkernstudent_kernel(tc, x, w1, w2, sh, d0, dx, og, base, out):
                 in_=op["bf16"][:].rearrange("p n j -> p (n j)"),
             )
 
-        def product(bank, g, w_op, x_ops, h):
-            rows = slice(ROWS * g, ROWS * (g + 1))
+        def products(jobs):
             for c in range(0, HALF, MM_N):
-                nc.tensor.matmul_mx(
-                    out=bank[:, h * HALF + c : h * HALF + c + MM_N],
-                    lhsT=w_op["codes"][rows, :].bitcast(FP8X4),
-                    lhsT_scale=w_op["scales"][rows, :],
-                    rhs=x_ops[h]["codes"][rows, c : c + MM_N].bitcast(FP8X4),
-                    rhs_scale=x_ops[h]["scales"][rows, c : c + MM_N],
-                    start=True,
-                    stop=True,
-                )
+                for banks, w_op, x_ops, g, h in jobs:
+                    rows = slice(ROWS * g, ROWS * (g + 1))
+                    nc.tensor.matmul_mx(
+                        out=banks[g][:, h * HALF + c : h * HALF + c + MM_N],
+                        lhsT=w_op["codes"][rows, :].bitcast(FP8X4),
+                        lhsT_scale=w_op["scales"][rows, :],
+                        rhs=x_ops[h]["codes"][rows, c : c + MM_N].bitcast(FP8X4),
+                        rhs_scale=x_ops[h]["scales"][rows, c : c + MM_N],
+                        start=True,
+                        stop=True,
+                    )
 
         xq = [operand("x%d" % h, HALF) for h in range(2)]
         dxq = [operand("dx%d" % h, HALF) for h in range(2)]
@@ -119,8 +120,8 @@ def tile_rows_tnkernstudent_kernel(tc, x, w1, w2, sh, d0, dx, og, base, out):
                 out=vec_rows[0:P:32, i * M : (i + 1) * M].rearrange("a (g i) -> a g i", i=32),
                 in_=vec.rearrange("g (a i) o -> a g (i o)", i=32),
             )
-        load_operand(w1q, w1, slice(0, M))
         load_operand(xq[1], x, halves[1])
+        load_operand(w1q, w1, slice(0, M))
         for i in range(2):
             nc.sync.dma_start(out=d0_pairs[i][:], in_=d0[2 * i : 2 * i + 2].rearrange("g m n -> m g n"))
         for h in range(2):
@@ -128,14 +129,17 @@ def tile_rows_tnkernstudent_kernel(tc, x, w1, w2, sh, d0, dx, og, base, out):
         for i in range(2):
             nc.sync.dma_start(out=base_pairs[i][:], in_=base[2 * i : 2 * i + 2].rearrange("g m n -> m g n"))
 
-        def z2_functions(g, cols):
-            z2 = bank_b[g][:, cols]
-            nc.scalar.activation(out=nsilu[g][:, cols], in_=z2, func=ACT.Silu, scale=-1.0)
-            nc.scalar.activation(out=tanh[g][:, cols], in_=z2, func=ACT.Tanh, scale=0.5)
-            nc.scalar.activation(out=silu[g][:, cols], in_=z2, func=ACT.Silu)
+        def make_nsilu(g, cols):
+            nc.scalar.activation(out=nsilu[g][:, cols], in_=bank_b[g][:, cols], func=ACT.Silu, scale=-1.0)
 
-        def make_e0(g):
-            nc.gpsimd.tensor_scalar(
+        def make_tanh(g, cols):
+            nc.scalar.activation(out=tanh[g][:, cols], in_=bank_b[g][:, cols], func=ACT.Tanh, scale=0.5)
+
+        def make_silu(g, cols):
+            nc.scalar.activation(out=silu[g][:, cols], in_=bank_b[g][:, cols], func=ACT.Silu)
+
+        def make_e0(engine, g):
+            engine.tensor_scalar(
                 out=e0[g][:], in0=d0_pairs[g // 2][:, g % 2, :], scalar1=sh_half[:, g : g + 1], scalar2=0.5,
                 op0=ALU.mult, op1=ALU.add,
             )
@@ -163,105 +167,137 @@ def tile_rows_tnkernstudent_kernel(tc, x, w1, w2, sh, d0, dx, og, base, out):
                 op0=ALU.mult, op1=ALU.mult,
             )
 
-        def make_ad(g):
-            nc.vector.tensor_tensor(out=ad[g][:], in0=a1[g][:], in1=a2[g][:], op=ALU.mult)
+        def make_ad(engine, g, cols):
+            engine.tensor_tensor(out=ad[g][:, cols], in0=a1[g][:, cols], in1=a2[g][:, cols], op=ALU.mult)
 
-        def make_total(g):
-            nc.vector.tensor_tensor(out=total[g][:], in0=ad[g][:], in1=bterm[g][:], op=ALU.add)
+        def make_total(engine, g, cols):
+            engine.tensor_tensor(out=total[g][:, cols], in0=ad[g][:, cols], in1=bterm[g][:, cols], op=ALU.add)
 
-        def make_scaled(g):
+        def make_scaled(g, cols):
             nc.vector.scalar_tensor_tensor(
-                out=scaled[g][:], in0=total[g][:], scalar=og_col(g), in1=inv2[g][:], op0=ALU.mult, op1=ALU.mult
+                out=scaled[g][:, cols], in0=total[g][:, cols], scalar=og_col(g), in1=inv2[g][:, cols],
+                op0=ALU.mult, op1=ALU.mult,
             )
 
-        def make_y(g):
-            nc.vector.tensor_tensor(out=y[g][:], in0=scaled[g][:], in1=base_pairs[g // 2][:, g % 2, :], op=ALU.add)
-            nc.sync.dma_start(out=out[g], in_=y[g][:])
+        def make_y(g, cols):
+            nc.vector.tensor_tensor(
+                out=y[g][:, cols], in0=scaled[g][:, cols], in1=base_pairs[g // 2][:, g % 2, cols], op=ALU.add
+            )
+            nc.sync.dma_start(out=out[g, :, cols], in_=y[g][:, cols])
 
+        def z1(groups, h):
+            return [(bank_a, w1q, xq, g, h) for g in groups]
+
+        def z2(groups, h):
+            return [(bank_b, w2q, xq, g, h) for g in groups]
+
+        def tz2(groups, h):
+            return [(bank_a, w2q, dxq, g, h) for g in groups]
+
+        def tz1(groups, h):
+            return [(bank_b, w1q, dxq, g, h) for g in groups]
+
+        def make_root(g):
+            nc.scalar.activation(out=root[g][:], in_=dn[g][:], func=ACT.Abs_reciprocal_sqrt, scale=2.0)
+
+        def make_inv(g, cols):
+            nc.scalar.activation(out=inv[g][:, cols], in_=root[g][:, cols], func=ACT.Square)
+
+        def make_inv2(g, cols):
+            nc.scalar.activation(out=inv2[g][:, cols], in_=inv[g][:, cols], func=ACT.Square)
+
+        left, right = halves
         interleave_v(xq[0])
         interleave_v(w2q)
         quantize(xq[0])
         quantize(w2q)
-        for g in range(G):
-            product(bank_b[g], g, w2q, xq, 0)
-        interleave_v(w1q)
+        products(z2(range(G), 0))
         nc.vector.transpose(vec_cols[:], vec_rows[:])
-        quantize(w1q)
-        nc.vector.tensor_scalar(out=sh_half[:], in0=vec_cols[:, 0:M:32], scalar1=0.5, scalar2=None, op0=ALU.mult)
-        for g in range(G):
-            product(bank_a[g], g, w1q, xq, 0)
-        z2_functions(0, halves[0])
-        z2_functions(1, halves[0])
         interleave_v(xq[1])
+        nc.vector.tensor_scalar(out=sh_half[:], in0=vec_cols[:, 0:M:32], scalar1=0.5, scalar2=None, op0=ALU.mult)
+        interleave_v(w1q)
         quantize(xq[1])
+        quantize(w1q)
+        make_nsilu(0, left)
+        for g in (1, 2, 3, 0):
+            make_tanh(g, left)
+        make_silu(0, left)
+        products(z2((1, 2), 1) + z1((0,), 0))
+        products(z1((0,), 1) + z2((3,), 1) + z1((1, 2), 0))
+        products(z1((1,), 1) + z2((0,), 1) + z1((2,), 1) + z1((3,), 0))
+        products(z1((3,), 1))
+        for g in (1, 2, 3, 0):
+            make_tanh(g, right)
+        make_nsilu(0, right)
+        make_silu(0, right)
         for g in range(2):
-            product(bank_a[g], g, w1q, xq, 1)
-        for g in range(G):
-            product(bank_b[g], g, w2q, xq, 1)
+            make_e0(nc.vector, g)
         for g in range(2, G):
-            product(bank_a[g], g, w1q, xq, 1)
-        z2_functions(0, halves[1])
-        z2_functions(1, halves[1])
+            make_e0(nc.gpsimd, g)
         for g in range(G):
-            make_e0(g)
-
-        make_dn(0)
-        make_dn(1)
-        make_a2(0)
-        make_dn(2)
-        make_dn(3)
+            make_dn(g)
         interleave_s(dxq[0])
         interleave_s(dxq[1])
-        z2_functions(2, whole)
-        z2_functions(3, whole)
-        quantize(dxq[0])
-        for g in range(2):
-            product(bank_a[g], g, w2q, dxq, 0)
-            product(bank_b[g], g, w1q, dxq, 0)
+        for g in range(1, G):
+            make_nsilu(g, whole)
+            make_silu(g, whole)
         make_a2(1)
-        make_a1(0, halves[0])
-        make_b(0, halves[0])
-        make_a1(1, halves[0])
+        quantize(dxq[0])
+        products(tz2(range(G), 0))
+        products(tz1((0,), 0))
+        make_a2(2)
+        make_a2(3)
         quantize(dxq[1])
-        make_b(1, halves[0])
-        for g in range(2):
-            product(bank_a[g], g, w2q, dxq, 1)
-            product(bank_b[g], g, w1q, dxq, 1)
+        products(tz2((1, 2, 3), 1))
+        make_a1(0, left)
+        make_b(0, left)
+        products(tz2((0,), 1))
+        products(tz1((0,), 1) + tz1((1,), 0))
+        products(tz1((1,), 1))
         for g in range(2, G):
             for h in range(2):
-                product(bank_a[g], g, w2q, dxq, h)
-        for g in range(2, G):
-            for h in range(2):
-                product(bank_b[g], g, w1q, dxq, h)
-        for g in range(2):
-            make_a1(g, halves[1])
-            make_b(g, halves[1])
+                products(tz1((g,), h))
+        make_a2(0)
 
-        for pair in ((0, 1), (2, 3)):
-            for g in pair:
-                nc.scalar.activation(out=root[g][:], in_=dn[g][:], func=ACT.Abs_reciprocal_sqrt, scale=2.0)
-            for g in pair:
-                nc.scalar.activation(out=inv[g][:], in_=root[g][:], func=ACT.Square)
-            for g in pair:
-                nc.scalar.activation(out=inv2[g][:], in_=inv[g][:], func=ACT.Square)
+        make_root(0)
+        make_root(1)
+        make_inv(0, whole)
+        make_inv(1, whole)
+        make_inv2(0, whole)
+        make_root(2)
+        make_inv2(1, whole)
+        make_inv(2, whole)
+        make_root(3)
+        make_inv2(2, whole)
+        for cols in halves:
+            make_inv(3, cols)
+        for cols in halves:
+            make_inv2(3, cols)
 
-        make_ad(0)
-        make_ad(1)
-        make_total(0)
-        make_total(1)
-        for g in range(2, G):
-            make_a2(g)
-            make_a1(g, whole)
-            make_b(g, whole)
-        make_ad(2)
-        make_scaled(0)
-        make_ad(3)
-        make_y(0)
-        make_total(2)
-        make_scaled(1)
-        make_total(3)
-        make_y(1)
-        make_scaled(2)
-        make_scaled(3)
-        make_y(2)
-        make_y(3)
+        make_a1(1, whole)
+        make_a1(0, right)
+        make_b(0, right)
+        for cols in halves:
+            make_ad(nc.gpsimd, 0, cols)
+            make_ad(nc.gpsimd, 1, cols)
+            make_total(nc.gpsimd, 0, cols)
+        make_a1(2, whole)
+        make_b(1, whole)
+        make_a1(3, whole)
+        make_b(2, whole)
+        make_b(3, whole)
+        make_ad(nc.vector, 2, whole)
+        make_total(nc.vector, 1, whole)
+        make_ad(nc.vector, 3, whole)
+        make_total(nc.vector, 2, whole)
+        make_scaled(0, whole)
+        make_total(nc.vector, 3, whole)
+        make_scaled(1, whole)
+        make_y(0, whole)
+        make_y(1, whole)
+        make_scaled(2, whole)
+        make_scaled(3, left)
+        make_y(2, whole)
+        make_scaled(3, right)
+        make_y(3, left)
+        make_y(3, right)

@@ -45,17 +45,17 @@ def tile_rows_tnkernstudent_kernel(tc, x, w1, w2, sh, d0, dx, og, base, out):
         def load_operand(op, src, cols):
             nc.sync.dma_start(out=op["raw"][:], in_=src.rearrange("g (p j) n -> (g p) j n", j=PACK)[:, :, cols])
 
-        def interleave_views(op):
-            dst = op["bf16"][:].rearrange("p (c i) j -> p c j i", i=RUN)
-            src = op["raw"][:].rearrange("p j (c i) -> p c j i", i=RUN)
+        def interleave_views(op, cols):
+            dst = op["bf16"][:, cols, :].rearrange("p (c i) j -> p c j i", i=RUN)
+            src = op["raw"][:, :, cols].rearrange("p j (c i) -> p c j i", i=RUN)
             return dst, src
 
-        def interleave_v(op):
-            dst, src = interleave_views(op)
+        def interleave_v(op, cols=slice(None)):
+            dst, src = interleave_views(op, cols)
             nc.vector.tensor_copy(out=dst, in_=src)
 
-        def interleave_s(op):
-            dst, src = interleave_views(op)
+        def interleave_s(op, cols=slice(None)):
+            dst, src = interleave_views(op, cols)
             nc.scalar.copy(out=dst, in_=src)
 
         def quantize(op):
@@ -114,14 +114,14 @@ def tile_rows_tnkernstudent_kernel(tc, x, w1, w2, sh, d0, dx, og, base, out):
 
         nc.gpsimd.memset(vec_rows[:], 0.0)
         load_operand(xq[0], x, halves[0])
-        load_operand(w2q, w2, slice(0, M))
         for i, vec in enumerate((sh, og)):
             nc.sync.dma_start(
                 out=vec_rows[0:P:32, i * M : (i + 1) * M].rearrange("a (g i) -> a g i", i=32),
                 in_=vec.rearrange("g (a i) o -> a g (i o)", i=32),
             )
-        load_operand(xq[1], x, halves[1])
+        load_operand(w2q, w2, slice(0, M))
         load_operand(w1q, w1, slice(0, M))
+        load_operand(xq[1], x, halves[1])
         for i in range(2):
             nc.sync.dma_start(out=d0_pairs[i][:], in_=d0[2 * i : 2 * i + 2].rearrange("g m n -> m g n"))
         for h in range(2):
@@ -212,41 +212,46 @@ def tile_rows_tnkernstudent_kernel(tc, x, w1, w2, sh, d0, dx, og, base, out):
         quantize(xq[0])
         quantize(w2q)
         products(z2(range(G), 0))
+        interleave_v(w1q)
         nc.vector.transpose(vec_cols[:], vec_rows[:])
+        quantize(w1q)
+        products(z1(range(G), 0))
         interleave_v(xq[1])
         nc.vector.tensor_scalar(out=sh_half[:], in0=vec_cols[:, 0:M:32], scalar1=0.5, scalar2=None, op0=ALU.mult)
-        interleave_v(w1q)
         quantize(xq[1])
-        quantize(w1q)
         make_nsilu(0, left)
-        for g in (1, 2, 3, 0):
+        for g in (2, 3, 0, 1):
             make_tanh(g, left)
         make_silu(0, left)
-        products(z2((1, 2), 1) + z1((0,), 0))
-        products(z1((0,), 1) + z2((3,), 1) + z1((1, 2), 0))
-        products(z1((1,), 1) + z2((0,), 1) + z1((2,), 1) + z1((3,), 0))
-        products(z1((3,), 1))
-        for g in (1, 2, 3, 0):
+        make_nsilu(1, left)
+        make_silu(1, left)
+        products(z1((0, 1), 1))
+        products(z2((2, 3, 0), 1))
+        products(z1((2, 3), 1) + z2((1,), 1))
+        for g in (2, 3, 0, 1):
             make_tanh(g, right)
-        make_nsilu(0, right)
-        make_silu(0, right)
         for g in range(2):
             make_e0(nc.vector, g)
         for g in range(2, G):
             make_e0(nc.gpsimd, g)
         for g in range(G):
             make_dn(g)
-        interleave_s(dxq[0])
+        interleave_s(dxq[0], slice(128, HALF))
+        interleave_v(dxq[0], slice(0, 128))
+        make_nsilu(0, right)
+        make_silu(0, right)
         interleave_s(dxq[1])
-        for g in range(1, G):
+        make_nsilu(1, right)
+        make_silu(1, right)
+        for g in range(2, G):
             make_nsilu(g, whole)
             make_silu(g, whole)
-        make_a2(1)
+        make_a2(2)
         quantize(dxq[0])
         products(tz2(range(G), 0))
         products(tz1((0,), 0))
-        make_a2(2)
         make_a2(3)
+        make_a2(1)
         quantize(dxq[1])
         products(tz2((1, 2, 3), 1))
         make_a1(0, left)
@@ -277,16 +282,18 @@ def tile_rows_tnkernstudent_kernel(tc, x, w1, w2, sh, d0, dx, og, base, out):
         make_a1(1, whole)
         make_a1(0, right)
         make_b(0, right)
-        for cols in halves:
-            make_ad(nc.gpsimd, 0, cols)
-            make_ad(nc.gpsimd, 1, cols)
-            make_total(nc.gpsimd, 0, cols)
+        make_ad(nc.gpsimd, 0, left)
+        make_ad(nc.gpsimd, 1, left)
+        make_total(nc.gpsimd, 0, left)
+        make_ad(nc.gpsimd, 0, right)
+        make_ad(nc.gpsimd, 1, right)
         make_a1(2, whole)
         make_b(1, whole)
         make_a1(3, whole)
         make_b(2, whole)
         make_b(3, whole)
         make_ad(nc.vector, 2, whole)
+        make_total(nc.vector, 0, right)
         make_total(nc.vector, 1, whole)
         make_ad(nc.vector, 3, whole)
         make_total(nc.vector, 2, whole)

@@ -19,11 +19,14 @@ ROWS = D // PACK
 HALF = N // 2
 MM_N = 128
 RUN = 4
+BLOCK = 32
+DX_ON_VECTOR = 128
 
 
 def tile_rows_tnkernstudent_kernel(tc, x, w1, w2, sh, d0, dx, og, base, out):
     nc = tc.nc
     halves = [slice(0, HALF), slice(HALF, N)]
+    left, right = halves
     whole = slice(0, N)
 
     with ExitStack() as ctx:
@@ -50,11 +53,11 @@ def tile_rows_tnkernstudent_kernel(tc, x, w1, w2, sh, d0, dx, og, base, out):
             src = op["raw"][:, :, cols].rearrange("p j (c i) -> p c j i", i=RUN)
             return dst, src
 
-        def interleave_v(op, cols=slice(None)):
+        def interleave_on_vector(op, cols=slice(None)):
             dst, src = interleave_views(op, cols)
             nc.vector.tensor_copy(out=dst, in_=src)
 
-        def interleave_s(op, cols=slice(None)):
+        def interleave_on_scalar(op, cols=slice(None)):
             dst, src = interleave_views(op, cols)
             nc.scalar.copy(out=dst, in_=src)
 
@@ -107,27 +110,22 @@ def tile_rows_tnkernstudent_kernel(tc, x, w1, w2, sh, d0, dx, og, base, out):
         y = per_group("y")
 
         def sh_col(g):
-            return vec_cols[:, 32 * g : 32 * g + 1]
+            return vec_cols[:, BLOCK * g : BLOCK * g + 1]
 
         def og_col(g):
-            return vec_cols[:, M + 32 * g : M + 32 * g + 1]
+            return vec_cols[:, M + BLOCK * g : M + BLOCK * g + 1]
 
-        nc.gpsimd.memset(vec_rows[:], 0.0)
-        load_operand(xq[0], x, halves[0])
-        for i, vec in enumerate((sh, og)):
-            nc.sync.dma_start(
-                out=vec_rows[0:P:32, i * M : (i + 1) * M].rearrange("a (g i) -> a g i", i=32),
-                in_=vec.rearrange("g (a i) o -> a g (i o)", i=32),
-            )
-        load_operand(w2q, w2, slice(0, M))
-        load_operand(w1q, w1, slice(0, M))
-        load_operand(xq[1], x, halves[1])
-        for i in range(2):
-            nc.sync.dma_start(out=d0_pairs[i][:], in_=d0[2 * i : 2 * i + 2].rearrange("g m n -> m g n"))
-        for h in range(2):
-            load_operand(dxq[h], dx, halves[h])
-        for i in range(2):
-            nc.sync.dma_start(out=base_pairs[i][:], in_=base[2 * i : 2 * i + 2].rearrange("g m n -> m g n"))
+        def z1(groups, h):
+            return [(bank_a, w1q, xq, g, h) for g in groups]
+
+        def z2(groups, h):
+            return [(bank_b, w2q, xq, g, h) for g in groups]
+
+        def tz2(groups, h):
+            return [(bank_a, w2q, dxq, g, h) for g in groups]
+
+        def tz1(groups, h):
+            return [(bank_b, w1q, dxq, g, h) for g in groups]
 
         def make_nsilu(g, cols):
             nc.scalar.activation(out=nsilu[g][:, cols], in_=bank_b[g][:, cols], func=ACT.Silu, scale=-1.0)
@@ -161,7 +159,7 @@ def tile_rows_tnkernstudent_kernel(tc, x, w1, w2, sh, d0, dx, og, base, out):
                 op0=ALU.subtract, op1=ALU.mult,
             )
 
-        def make_b(g, cols):
+        def make_bterm(g, cols):
             nc.vector.scalar_tensor_tensor(
                 out=bterm[g][:, cols], in0=bank_b[g][:, cols], scalar=sh_col(g), in1=silu[g][:, cols],
                 op0=ALU.mult, op1=ALU.mult,
@@ -173,30 +171,6 @@ def tile_rows_tnkernstudent_kernel(tc, x, w1, w2, sh, d0, dx, og, base, out):
         def make_total(engine, g, cols):
             engine.tensor_tensor(out=total[g][:, cols], in0=ad[g][:, cols], in1=bterm[g][:, cols], op=ALU.add)
 
-        def make_scaled(g, cols):
-            nc.vector.scalar_tensor_tensor(
-                out=scaled[g][:, cols], in0=total[g][:, cols], scalar=og_col(g), in1=inv2[g][:, cols],
-                op0=ALU.mult, op1=ALU.mult,
-            )
-
-        def make_y(g, cols):
-            nc.vector.tensor_tensor(
-                out=y[g][:, cols], in0=scaled[g][:, cols], in1=base_pairs[g // 2][:, g % 2, cols], op=ALU.add
-            )
-            nc.sync.dma_start(out=out[g, :, cols], in_=y[g][:, cols])
-
-        def z1(groups, h):
-            return [(bank_a, w1q, xq, g, h) for g in groups]
-
-        def z2(groups, h):
-            return [(bank_b, w2q, xq, g, h) for g in groups]
-
-        def tz2(groups, h):
-            return [(bank_a, w2q, dxq, g, h) for g in groups]
-
-        def tz1(groups, h):
-            return [(bank_b, w1q, dxq, g, h) for g in groups]
-
         def make_root(g):
             nc.scalar.activation(out=root[g][:], in_=dn[g][:], func=ACT.Abs_reciprocal_sqrt, scale=2.0)
 
@@ -206,21 +180,51 @@ def tile_rows_tnkernstudent_kernel(tc, x, w1, w2, sh, d0, dx, og, base, out):
         def make_inv2(g, cols):
             nc.scalar.activation(out=inv2[g][:, cols], in_=inv[g][:, cols], func=ACT.Square)
 
-        left, right = halves
-        interleave_v(xq[0])
-        interleave_v(w2q)
+        def make_scaled(g, cols):
+            nc.vector.scalar_tensor_tensor(
+                out=scaled[g][:, cols], in0=total[g][:, cols], scalar=og_col(g), in1=inv2[g][:, cols],
+                op0=ALU.mult, op1=ALU.mult,
+            )
+
+        def make_y_and_store(g, cols):
+            nc.vector.tensor_tensor(
+                out=y[g][:, cols], in0=scaled[g][:, cols], in1=base_pairs[g // 2][:, g % 2, cols], op=ALU.add
+            )
+            nc.sync.dma_start(out=out[g, :, cols], in_=y[g][:, cols])
+
+        nc.gpsimd.memset(vec_rows[:], 0.0)
+        load_operand(xq[0], x, left)
+        for i, vec in enumerate((sh, og)):
+            nc.sync.dma_start(
+                out=vec_rows[0:P:BLOCK, i * M : (i + 1) * M].rearrange("a (g i) -> a g i", i=BLOCK),
+                in_=vec.rearrange("g (a i) o -> a g (i o)", i=BLOCK),
+            )
+        load_operand(w2q, w2, slice(0, M))
+        load_operand(w1q, w1, slice(0, M))
+        load_operand(xq[1], x, right)
+        for i in range(2):
+            nc.sync.dma_start(out=d0_pairs[i][:], in_=d0[2 * i : 2 * i + 2].rearrange("g m n -> m g n"))
+        for h in range(2):
+            load_operand(dxq[h], dx, halves[h])
+        for i in range(2):
+            nc.sync.dma_start(out=base_pairs[i][:], in_=base[2 * i : 2 * i + 2].rearrange("g m n -> m g n"))
+
+        interleave_on_vector(xq[0])
+        interleave_on_vector(w2q)
         quantize(xq[0])
         quantize(w2q)
         products(z2(range(G), 0))
-        interleave_v(w1q)
+        interleave_on_vector(w1q)
         nc.vector.transpose(vec_cols[:], vec_rows[:])
         quantize(w1q)
         products(z1(range(G), 0))
-        interleave_v(xq[1])
-        nc.vector.tensor_scalar(out=sh_half[:], in0=vec_cols[:, 0:M:32], scalar1=0.5, scalar2=None, op0=ALU.mult)
+        interleave_on_vector(xq[1])
+        nc.vector.tensor_scalar(out=sh_half[:], in0=vec_cols[:, 0:M:BLOCK], scalar1=0.5, scalar2=None, op0=ALU.mult)
         quantize(xq[1])
+
+        tanh_order = (2, 3, 0, 1)
         make_nsilu(0, left)
-        for g in (2, 3, 0, 1):
+        for g in tanh_order:
             make_tanh(g, left)
         make_silu(0, left)
         make_nsilu(1, left)
@@ -228,24 +232,27 @@ def tile_rows_tnkernstudent_kernel(tc, x, w1, w2, sh, d0, dx, og, base, out):
         products(z1((0, 1), 1))
         products(z2((2, 3, 0), 1))
         products(z1((2, 3), 1) + z2((1,), 1))
-        for g in (2, 3, 0, 1):
+        for g in tanh_order:
             make_tanh(g, right)
+
         for g in range(2):
             make_e0(nc.vector, g)
         for g in range(2, G):
             make_e0(nc.gpsimd, g)
         for g in range(G):
             make_dn(g)
-        interleave_s(dxq[0], slice(128, HALF))
-        interleave_v(dxq[0], slice(0, 128))
+
+        interleave_on_scalar(dxq[0], slice(DX_ON_VECTOR, HALF))
+        interleave_on_vector(dxq[0], slice(0, DX_ON_VECTOR))
         make_nsilu(0, right)
         make_silu(0, right)
-        interleave_s(dxq[1])
+        interleave_on_scalar(dxq[1])
         make_nsilu(1, right)
         make_silu(1, right)
         for g in range(2, G):
             make_nsilu(g, whole)
             make_silu(g, whole)
+
         make_a2(2)
         quantize(dxq[0])
         products(tz2(range(G), 0))
@@ -255,7 +262,7 @@ def tile_rows_tnkernstudent_kernel(tc, x, w1, w2, sh, d0, dx, og, base, out):
         quantize(dxq[1])
         products(tz2((1, 2, 3), 1))
         make_a1(0, left)
-        make_b(0, left)
+        make_bterm(0, left)
         products(tz2((0,), 1))
         products(tz1((0,), 1) + tz1((1,), 0))
         products(tz1((1,), 1))
@@ -281,17 +288,17 @@ def tile_rows_tnkernstudent_kernel(tc, x, w1, w2, sh, d0, dx, og, base, out):
 
         make_a1(1, whole)
         make_a1(0, right)
-        make_b(0, right)
+        make_bterm(0, right)
         make_ad(nc.gpsimd, 0, left)
-        make_ad(nc.gpsimd, 1, left)
-        make_total(nc.gpsimd, 0, left)
+        make_ad(nc.gpsimd, 1, whole)
         make_ad(nc.gpsimd, 0, right)
-        make_ad(nc.gpsimd, 1, right)
+        make_total(nc.gpsimd, 0, left)
         make_a1(2, whole)
-        make_b(1, whole)
+        make_bterm(1, whole)
         make_a1(3, whole)
-        make_b(2, whole)
-        make_b(3, whole)
+        make_bterm(2, whole)
+        make_bterm(3, whole)
+
         make_ad(nc.vector, 2, whole)
         make_total(nc.vector, 0, right)
         make_total(nc.vector, 1, whole)
@@ -300,11 +307,11 @@ def tile_rows_tnkernstudent_kernel(tc, x, w1, w2, sh, d0, dx, og, base, out):
         make_scaled(0, whole)
         make_total(nc.vector, 3, whole)
         make_scaled(1, whole)
-        make_y(0, whole)
-        make_y(1, whole)
+        make_y_and_store(0, whole)
+        make_y_and_store(1, whole)
         make_scaled(2, whole)
         make_scaled(3, left)
-        make_y(2, whole)
+        make_y_and_store(2, whole)
         make_scaled(3, right)
-        make_y(3, left)
-        make_y(3, right)
+        for cols in halves:
+            make_y_and_store(3, cols)

from contextlib import ExitStack

import concourse.mybir as mybir

G, D, M, N = 4, 128, 128, 512
FLOPS = 4 * 2 * G * D * M * N

F32 = mybir.dt.float32
BF16 = mybir.dt.bfloat16
U32 = mybir.dt.uint32
U8 = mybir.dt.uint8
FP8X4 = mybir.dt.float8_e4m3fn_x4
ACT = mybir.ActivationFunctionType
ALU = mybir.AluOpType

P = 128
PACK = 4
ROWS = D // PACK
HALF = N // 2
MM_N = 128
RUN = 4
BLOCK = 32
DX_ON_VECTOR = 128


def tile_rows_tnkernstudent_kernel(tc, x, w1, w2, sh, d0, dx, og, base, out):
    nc = tc.nc
    halves = [slice(0, HALF), slice(HALF, N)]
    left, right = halves
    whole = slice(0, N)

    with ExitStack() as ctx:
        sb = ctx.enter_context(tc.tile_pool(name="sb", bufs=1))
        ps = ctx.enter_context(tc.psum_pool(name="ps", bufs=1))
        ctx.enter_context(tc.manual_schedule())

        def per_group(name):
            return [sb.tile([P, N], F32, name="%s%d" % (name, g)) for g in range(G)]

        def operand(name, width):
            return {
                "raw": sb.tile([P, PACK, width], F32, name=name + "_raw", align_bytes=64),
                "bf16": sb.tile([P, width, PACK], BF16, name=name + "_bf16", align_bytes=64),
                "codes": sb.tile([P, width], U32, name=name + "_codes", align_bytes=64),
                "scales": sb.tile([P, width], U8, name=name + "_scales", align_bytes=64),
            }

        def load_operand(op, src, cols):
            nc.sync.dma_start(out=op["raw"][:], in_=src.rearrange("g (p j) n -> (g p) j n", j=PACK)[:, :, cols])

        def interleave_views(op, cols):
            dst = op["bf16"][:, cols, :].rearrange("p (c i) j -> p c j i", i=RUN)
            src = op["raw"][:, :, cols].rearrange("p j (c i) -> p c j i", i=RUN)
            return dst, src

        def interleave_on_vector(op, cols=slice(None)):
            dst, src = interleave_views(op, cols)
            nc.vector.tensor_copy(out=dst, in_=src)

        def interleave_on_scalar(op, cols=slice(None)):
            dst, src = interleave_views(op, cols)
            nc.scalar.copy(out=dst, in_=src)

        def quantize(op):
            nc.vector.quantize_mx(
                out=op["codes"][:].bitcast(FP8X4),
                scales=op["scales"][:],
                in_=op["bf16"][:].rearrange("p n j -> p (n j)"),
            )

        def products(jobs):
            for c in range(0, HALF, MM_N):
                for banks, w_op, x_ops, g, h in jobs:
                    rows = slice(ROWS * g, ROWS * (g + 1))
                    nc.tensor.matmul_mx(
                        out=banks[g][:, h * HALF + c : h * HALF + c + MM_N],
                        lhsT=w_op["codes"][rows, :].bitcast(FP8X4),
                        lhsT_scale=w_op["scales"][rows, :],
                        rhs=x_ops[h]["codes"][rows, c : c + MM_N].bitcast(FP8X4),
                        rhs_scale=x_ops[h]["scales"][rows, c : c + MM_N],
                        start=True,
                        stop=True,
                    )

        xq = [operand("x%d" % h, HALF) for h in range(2)]
        dxq = [operand("dx%d" % h, HALF) for h in range(2)]
        w1q = operand("w1", M)
        w2q = operand("w2", M)
        bank_a = [ps.tile([P, N], F32, name="bank_a%d" % g) for g in range(G)]
        bank_b = [ps.tile([P, N], F32, name="bank_b%d" % g) for g in range(G)]
        d0_pairs = [sb.tile([P, 2, N], F32, name="d0_pair%d" % i) for i in range(2)]
        base_pairs = [sb.tile([P, 2, N], F32, name="base_pair%d" % i) for i in range(2)]
        vec_rows = sb.tile([P, 2 * M], F32, name="vec_rows", align_bytes=64)
        vec_cols = sb.tile([P, 2 * M], F32, name="vec_cols", align_bytes=64)
        sh_half = sb.tile([P, G], F32, name="sh_half")
        e0 = per_group("e0")
        dn = per_group("dn")
        nsilu = per_group("nsilu")
        tanh = per_group("tanh")
        silu = per_group("silu")
        a1 = per_group("a1")
        a2 = per_group("a2")
        bterm = per_group("bterm")
        root = per_group("root")
        inv = per_group("inv")
        inv2 = per_group("inv2")
        ad = per_group("ad")
        total = per_group("total")
        scaled = per_group("scaled")
        y = per_group("y")

        def sh_col(g):
            return vec_cols[:, BLOCK * g : BLOCK * g + 1]

        def og_col(g):
            return vec_cols[:, M + BLOCK * g : M + BLOCK * g + 1]

        def z1(groups, h):
            return [(bank_a, w1q, xq, g, h) for g in groups]

        def z2(groups, h):
            return [(bank_b, w2q, xq, g, h) for g in groups]

        def tz2(groups, h):
            return [(bank_a, w2q, dxq, g, h) for g in groups]

        def tz1(groups, h):
            return [(bank_b, w1q, dxq, g, h) for g in groups]

        def make_nsilu(g, cols):
            nc.scalar.activation(out=nsilu[g][:, cols], in_=bank_b[g][:, cols], func=ACT.Silu, scale=-1.0)

        def make_tanh(g, cols):
            nc.scalar.activation(out=tanh[g][:, cols], in_=bank_b[g][:, cols], func=ACT.Tanh, scale=0.5)

        def make_silu(g, cols):
            nc.scalar.activation(out=silu[g][:, cols], in_=bank_b[g][:, cols], func=ACT.Silu)

        def make_e0(engine, g):
            engine.tensor_scalar(
                out=e0[g][:], in0=d0_pairs[g // 2][:, g % 2, :], scalar1=sh_half[:, g : g + 1], scalar2=0.5,
                op0=ALU.mult, op1=ALU.add,
            )

        def make_dn(g):
            nc.vector.scalar_tensor_tensor(
                out=dn[g][:], in0=bank_a[g][:], scalar=sh_half[:, g : g + 1], in1=e0[g][:],
                op0=ALU.mult, op1=ALU.subtract,
            )

        def make_a2(g):
            nc.vector.scalar_tensor_tensor(
                out=a2[g][:], in0=tanh[g][:], scalar=1.0, in1=dn[g][:], op0=ALU.add, op1=ALU.mult
            )

        def make_a1(g, cols):
            nc.vector.scalar_tensor_tensor(
                out=a1[g][:, cols], in0=nsilu[g][:, cols], scalar=1.0, in1=bank_a[g][:, cols],
                op0=ALU.subtract, op1=ALU.mult,
            )

        def make_bterm(g, cols):
            nc.vector.scalar_tensor_tensor(
                out=bterm[g][:, cols], in0=bank_b[g][:, cols], scalar=sh_col(g), in1=silu[g][:, cols],
                op0=ALU.mult, op1=ALU.mult,
            )

        def make_ad(engine, g, cols):
            engine.tensor_tensor(out=ad[g][:, cols], in0=a1[g][:, cols], in1=a2[g][:, cols], op=ALU.mult)

        def make_total(engine, g, cols):
            engine.tensor_tensor(out=total[g][:, cols], in0=ad[g][:, cols], in1=bterm[g][:, cols], op=ALU.add)

        def make_root(g):
            nc.scalar.activation(out=root[g][:], in_=dn[g][:], func=ACT.Abs_reciprocal_sqrt, scale=2.0)

        def make_inv(g, cols):
            nc.scalar.activation(out=inv[g][:, cols], in_=root[g][:, cols], func=ACT.Square)

        def make_inv2(g, cols):
            nc.scalar.activation(out=inv2[g][:, cols], in_=inv[g][:, cols], func=ACT.Square)

        def make_scaled(g, cols):
            nc.vector.scalar_tensor_tensor(
                out=scaled[g][:, cols], in0=total[g][:, cols], scalar=og_col(g), in1=inv2[g][:, cols],
                op0=ALU.mult, op1=ALU.mult,
            )

        def make_y_and_store(g, cols):
            nc.vector.tensor_tensor(
                out=y[g][:, cols], in0=scaled[g][:, cols], in1=base_pairs[g // 2][:, g % 2, cols], op=ALU.add
            )
            nc.sync.dma_start(out=out[g, :, cols], in_=y[g][:, cols])

        nc.gpsimd.memset(vec_rows[:], 0.0)
        load_operand(xq[0], x, left)
        for i, vec in enumerate((sh, og)):
            nc.sync.dma_start(
                out=vec_rows[0:P:BLOCK, i * M : (i + 1) * M].rearrange("a (g i) -> a g i", i=BLOCK),
                in_=vec.rearrange("g (a i) o -> a g (i o)", i=BLOCK),
            )
        load_operand(w2q, w2, slice(0, M))
        load_operand(w1q, w1, slice(0, M))
        load_operand(xq[1], x, right)
        for i in range(2):
            nc.sync.dma_start(out=d0_pairs[i][:], in_=d0[2 * i : 2 * i + 2].rearrange("g m n -> m g n"))
        for h in range(2):
            load_operand(dxq[h], dx, halves[h])
        for i in range(2):
            nc.sync.dma_start(out=base_pairs[i][:], in_=base[2 * i : 2 * i + 2].rearrange("g m n -> m g n"))

        interleave_on_vector(xq[0])
        interleave_on_vector(w2q)
        quantize(xq[0])
        quantize(w2q)
        products(z2(range(G), 0))
        interleave_on_vector(w1q)
        nc.vector.transpose(vec_cols[:], vec_rows[:])
        quantize(w1q)
        products(z1(range(G), 0))
        interleave_on_vector(xq[1])
        nc.vector.tensor_scalar(out=sh_half[:], in0=vec_cols[:, 0:M:BLOCK], scalar1=0.5, scalar2=None, op0=ALU.mult)
        quantize(xq[1])

        tanh_order = (2, 3, 0, 1)
        make_nsilu(0, left)
        for g in tanh_order:
            make_tanh(g, left)
        make_silu(0, left)
        make_nsilu(1, left)
        make_silu(1, left)
        products(z1((0, 1), 1))
        products(z2((2, 3, 0), 1))
        products(z1((2, 3), 1) + z2((1,), 1))
        for g in tanh_order:
            make_tanh(g, right)

        for g in range(2):
            make_e0(nc.vector, g)
        for g in range(2, G):
            make_e0(nc.gpsimd, g)
        for g in range(G):
            make_dn(g)

        interleave_on_scalar(dxq[0], slice(DX_ON_VECTOR, HALF))
        interleave_on_vector(dxq[0], slice(0, DX_ON_VECTOR))
        make_nsilu(0, right)
        make_silu(0, right)
        interleave_on_scalar(dxq[1])
        make_nsilu(1, right)
        make_silu(1, right)
        for g in range(2, G):
            make_nsilu(g, whole)
            make_silu(g, whole)

        make_a2(2)
        quantize(dxq[0])
        products(tz2(range(G), 0))
        products(tz1((0,), 0))
        make_a2(3)
        make_a2(1)
        quantize(dxq[1])
        products(tz2((1, 2, 3), 1))
        make_a1(0, left)
        make_bterm(0, left)
        products(tz2((0,), 1))
        products(tz1((0,), 1) + tz1((1,), 0))
        products(tz1((1,), 1))
        for g in range(2, G):
            for h in range(2):
                products(tz1((g,), h))
        make_a2(0)

        make_root(0)
        make_root(1)
        make_inv(0, whole)
        make_inv(1, whole)
        make_inv2(0, whole)
        make_root(2)
        make_inv2(1, whole)
        make_inv(2, whole)
        make_root(3)
        make_inv2(2, whole)
        for cols in halves:
            make_inv(3, cols)
        for cols in halves:
            make_inv2(3, cols)

        make_a1(1, whole)
        make_a1(0, right)
        make_bterm(0, right)
        make_ad(nc.gpsimd, 0, left)
        make_ad(nc.gpsimd, 1, whole)
        make_ad(nc.gpsimd, 0, right)
        make_total(nc.gpsimd, 0, left)
        make_a1(2, whole)
        make_bterm(1, whole)
        make_a1(3, whole)
        make_bterm(2, whole)
        make_bterm(3, whole)

        make_ad(nc.vector, 2, whole)
        make_total(nc.vector, 0, right)
        make_total(nc.vector, 1, whole)
        make_ad(nc.vector, 3, whole)
        make_total(nc.vector, 2, whole)
        make_scaled(0, whole)
        make_total(nc.vector, 3, whole)
        make_scaled(1, whole)
        make_y_and_store(0, whole)
        make_y_and_store(1, whole)
        make_scaled(2, whole)
        make_scaled(3, left)
        make_y_and_store(2, whole)
        make_scaled(3, right)
        for cols in halves:
            make_y_and_store(3, cols)
